import numpy as np
import ml_dtypes


def mxq(x, axis, fmt="e4m3"):
    dtype, down = {"e4m3": (ml_dtypes.float8_e4m3fn, 7), "e5m2": (ml_dtypes.float8_e5m2, 14)}[fmt]
    v = np.moveaxis(np.asarray(x, np.float32).astype(ml_dtypes.bfloat16).astype(np.float64), axis, -1)
    blocks = v.reshape(v.shape[:-1] + (-1, 32))
    amax = np.abs(blocks).max(-1, keepdims=True)
    byte = np.maximum(np.where(amax > 0, np.frexp(amax)[1] - 1 + 127, 0) - down, 1)
    scale = np.exp2(byte - 127.0)
    codes = (blocks / scale).astype(np.float32).astype(dtype).astype(np.float64)
    return np.moveaxis((codes * scale).reshape(v.shape), -1, axis)


WIDE = False


def mx_kscale(k):
    if not WIDE:
        return np.ones(k)
    levels = np.array([24, -24, 12, -12, 0])
    if k % 512:
        return np.exp2(np.random.permutation(np.resize(levels, k // 32))).repeat(32)
    a = np.empty((k // 512, 16))
    for p in range(k // 512):
        a[p, :8] = np.random.permutation(np.resize(levels, 8))
        for g in range(8):
            far = levels[np.abs(levels - a[p, g]) >= 10]
            a[p, g + 8] = far[np.random.randint(len(far))]
    return np.exp2(a.ravel()).repeat(32)


def f64(x):
    return np.asarray(x).astype(np.float64)


def striped(idx):
    return np.tile(idx.reshape(-1, 16).T, (8, 1)).astype(np.uint16)


def unstriped(offs):
    return offs[:16].T.reshape(-1).astype(np.int64)


E2M1 = np.array([0.0, 0.5, 1.0, 1.5, 2.0, 3.0, 4.0, 6.0, -0.0, -0.5, -1.0, -1.5, -2.0, -3.0, -4.0, -6.0])


def pack_weight(w, fmt):
    k, n = w.shape
    w = f64(np.asarray(w, np.float32).astype(ml_dtypes.bfloat16)).reshape(k // 32, 32, n)
    amax = np.abs(w).max(1)
    if fmt == "e4m3":
        byte = np.frexp(amax)[1] - 1 + 127 - 7
    else:
        mant, ex = np.frexp(amax / 6.0)
        byte = np.where(mant > 0.5, ex, ex - 1) + 127
    byte = np.clip(np.where(amax > 0, byte, 1), 1, 254)
    scaled = (w * np.exp2(127.0 - byte)[:, None, :]).reshape(k, n).astype(np.float32)
    by_word = np.ascontiguousarray(scaled.reshape(k // 512, 128, 4, n).transpose(0, 1, 3, 2))
    if fmt == "e4m3":
        words = by_word.astype(ml_dtypes.float8_e4m3fn).view(np.uint8)
    else:
        c = by_word.astype(ml_dtypes.float4_e2m1fn).view(np.uint8) & 0xF
        words = (c[..., 0::2] | (c[..., 1::2] << 4)).reshape(k // 512, 128, 2 * n)
    return np.ascontiguousarray(words), np.ascontiguousarray(byte.astype(np.uint8).reshape(k // 512, 16, n))


def unpack_weight(words, scales, fmt):
    g, _, n = scales.shape
    words = np.ascontiguousarray(words).reshape(g, 128, n, -1)
    if fmt == "e4m3":
        vals = words.view(ml_dtypes.float8_e4m3fn).astype(np.float64)
    else:
        nib = np.empty((g, 128, n, 4), np.uint8)
        nib[..., 0::2] = words & 0xF
        nib[..., 1::2] = words >> 4
        vals = E2M1[nib]
    vals = vals * np.repeat(np.exp2(scales.astype(np.float64) - 127.0), 8, axis=1)[..., None]
    return vals.transpose(0, 1, 3, 2).reshape(g * 512, n)


def pack_table4(v):
    words, scales = pack_weight(v, "e2m1")
    g, t = words.shape[0] // 2, v.shape[1]
    return np.ascontiguousarray(words.reshape(g, 2, 128, t, 2).transpose(0, 2, 3, 1, 4).reshape(g, 128, t, 4)), scales


def unpack_table4(words, scales):
    g, _, t, _ = words.shape
    return unpack_weight(words.reshape(g, 128, t, 2, 2).transpose(0, 3, 1, 2, 4).reshape(2 * g, 128, 2 * t), scales, "e2m1")


def planes(y):
    n, m = y.shape
    v = y.astype(np.float32).astype(ml_dtypes.bfloat16).astype(np.float64).reshape(n // 32, 32, m)
    top = np.abs(v).max(1)
    byte = np.clip(np.where(top > 0, np.frexp(top)[1] - 1 + 127 - 7, 1), 1, 254)
    codes = (v * np.exp2(127.0 - byte)[:, None, :]).reshape(n, m).astype(np.float32).astype(ml_dtypes.float8_e4m3fn).view(np.uint8)
    words = codes.reshape(n // 512, 128, 4, m).transpose(0, 1, 3, 2)
    return np.ascontiguousarray(words), np.ascontiguousarray(byte.astype(np.uint8).reshape(n // 512, 16, m))


def sigm(f):
    return 1.0 / (1.0 + np.exp(-np.maximum(f, -700.0)))


K, N, T, J = 1024, 512, 2048, 1024


def setup_inputs():
    n = np.random.standard_normal
    s = mx_kscale(K)[:, None]
    p_tab = pack_table4(n((K, T)) * s)
    return {
        "tab_words": p_tab[0],
        "tab_scales": p_tab[1],
        "wg": (n((K, N)) / np.sqrt(K) / s).astype(np.float32),
        "wh": (n((K, N)) / np.sqrt(K) / s).astype(np.float32),
        "bg": (0.3 * n(N) - 1.0).astype(np.float32),
        "rT": (n((N, T))).astype(np.float32),
        "offs": striped(np.random.permutation(T)[:J]),
    }


def reference(tab_words, tab_scales, wg, wh, bg, rT, offs):
    idx = unstriped(offs)
    tab_ = unpack_table4(tab_words, tab_scales)[:, idx]
    wg_ = mxq(f64(wg), 0, "e4m3")
    wh_ = mxq(f64(wh), 0, "e4m3")
    ga = wg_.T @ tab_
    gate = sigm(ga + f64(bg)[:, None])
    ha = wh_.T @ tab_
    out_0 = f64(rT)[:, idx] + gate * (np.tanh(ha) - f64(rT)[:, idx])
    return (out_0,) + planes(out_0)

@@ -1,0 +1,243 @@
+from contextlib import ExitStack
+
+import concourse.mybir as mybir
+
+K, N, T, J = 1024, 512, 2048, 1024
+FLOPS = 2 * 2 * K * N * J
+
+F32 = mybir.dt.float32
+BF16 = mybir.dt.bfloat16
+I32 = mybir.dt.int32
+U32 = mybir.dt.uint32
+U16 = mybir.dt.uint16
+U8 = mybir.dt.uint8
+FP8X4 = mybir.dt.float8_e4m3fn_x4
+FP4X4 = mybir.dt.float4_e2m1fn_x4
+ALU = mybir.AluOpType
+ACT = mybir.ActivationFunctionType
+
+P = 128
+PACK = 4
+PASSES = 2
+HALF = 512
+PIECES = ((0, 512), (512, 256), (768, 256))
+
+
+def tile_list_hwayt_tanhP_kernel(
+    tc, tab_words, tab_scales, wg, wh, bg, rT, offs, out_0, out_1, out_2
+):
+    nc = tc.nc
+    with ExitStack() as ctx:
+        keep = ctx.enter_context(tc.tile_pool(name="keep", bufs=1))
+        psum = ctx.enter_context(tc.psum_pool(name="psum", bufs=8))
+
+        def sb(shape, dtype, name, tag=None):
+            return keep.tile(shape, dtype, name=name, tag=tag or name, align_bytes=64)
+
+        offsets = keep.tile([P, J // 16], U16, name="offsets")
+        nc.sync.dma_start(offsets[:], offs)
+
+        scale_win = sb([P, T], U8, "scale_win")
+        for q in range(4):
+            nc.vector.memset(scale_win[32 * q : 32 * q + 24, :].bitcast(I32), 0)
+            nc.sync.dma_start(
+                scale_win[32 * q + 24 : 32 * q + 32, :].bitcast(I32),
+                tab_scales[:, 4 * q : 4 * q + 4, :].bitcast(I32),
+            )
+        planes = sb([P, PASSES * J], U8, "planes")
+        nc.gpsimd.memset(planes[:].bitcast(I32), 0)
+
+        word_win = sb([P, T], U32, "word_win")
+        nc.sync.dma_start(
+            word_win[:].bitcast(I32), tab_words[0].rearrange("p t b -> p (t b)").bitcast(I32)
+        )
+
+        def load_weight(w, a, name, tag=None):
+            raw = sb([P, PACK * N], F32, name, tag)
+            nc.sync.dma_start(
+                raw[:], w[512 * a : 512 * (a + 1), :].rearrange("(p i) n -> p (i n)", i=PACK)
+            )
+            return raw
+
+        r_rows = rT.rearrange("(p t) c -> p t c", t=PACK)
+
+        def load_r(t, tag):
+            win = sb([P, T], F32, "r_win%d" % t, tag)
+            nc.sync.dma_start(win[:], r_rows[:, t, :])
+            return win
+
+        wg_raw = [load_weight(wg, a, "wg_raw%d" % a) for a in range(PASSES)]
+        bias = sb([P, PACK], F32, "bias")
+        nc.scalar.dma_start(bias[:], bg.rearrange("(p t) -> p t", t=PACK))
+
+        neg_bias = sb([P, PACK], F32, "neg_bias")
+        nc.gpsimd.tensor_scalar(neg_bias[:], bias[:], -1.0, 0.0, ALU.mult, ALU.add)
+        warm = sb([P, 1], F32, "warm")
+        nc.scalar.activation(warm[:], bias[:, 0:1], ACT.Sigmoid)
+
+        picked_scales = sb([P, J], U8, "picked_scales")
+        nc.vector.tensor_copy(picked_scales[:], scale_win[:].indirect(offsets[:]))
+        for a in range(PASSES):
+            nc.sync.dma_start(
+                planes[0:100, a * J : (a + 1) * J].bitcast(I32),
+                picked_scales[24 + 4 * a : 124 + 4 * a, :].bitcast(I32),
+            )
+        r_win = [load_r(0, "scale_win")]
+
+        picked = sb([P, J], U32, "picked")
+        nc.vector.tensor_copy(picked[:], word_win[:].indirect(offsets[:]))
+        r_win.append(load_r(1, "word_win"))
+        parted = sb([P, PASSES * 2 * J], U8, "parted")
+        nc.vector.tensor_copy(
+            parted[:].bitcast(U16).rearrange("p (d j) -> p d j", d=PASSES),
+            picked[:].bitcast(U16).rearrange("p (j d) -> p d j", d=PASSES),
+        )
+        wh_raw = [load_weight(wh, 0, "wh_raw0", "picked")]
+
+        def round_pair(raw, u, on_scalar, name):
+            rounded = sb([P, 2 * P * PACK], BF16, name)
+            dst = rounded[:].rearrange("p (t m i) -> p m t i", t=2, i=PACK)
+            src = raw[:].rearrange("p (i m t) -> p m t i", i=PACK, t=PACK)[:, :, 2 * u : 2 * u + 2, :]
+            if on_scalar:
+                nc.scalar.copy(dst, src)
+            else:
+                nc.vector.tensor_copy(dst, src)
+            return rounded
+
+        def quantise_pair(rounded, name):
+            codes = sb([P, 2 * P], U32, name + "_codes")
+            scales = sb([P, 2 * P], U8, name + "_scales")
+            nc.vector.quantize_mx(out=codes[:].bitcast(FP8X4), scales=scales[:], in_=rounded[:])
+            return codes, scales
+
+        def quantise_weight(raw, name, scalar_share):
+            rounded = {
+                (a, u): round_pair(raw[a], u, 2 * a + u in scalar_share, "%s_bf%d%d" % (name, a, u))
+                for a in range(PASSES)
+                for u in range(2)
+            }
+            return {
+                (a, u): quantise_pair(rounded[(a, u)], "%s_q%d%d" % (name, a, u))
+                for a in range(PASSES)
+                for u in range(2)
+            }
+
+        def product(wq, t, c):
+            acc = psum.tile([P, HALF], F32, name="acc")
+            for a in range(PASSES):
+                codes, scales = wq[(a, t // 2)]
+                m = slice(P * (t % 2), P * (t % 2 + 1))
+                lo = 2 * (a * J + c * HALF)
+                nc.tensor.matmul_mx(
+                    out=acc[:],
+                    lhsT=codes[:, m].bitcast(FP8X4),
+                    lhsT_scale=scales[:, m],
+                    rhs=parted[:, lo : lo + 2 * HALF].bitcast(FP4X4),
+                    rhs_scale=planes[:, a * J + c * HALF : a * J + (c + 1) * HALF],
+                    start=(a == 0),
+                    stop=(a == PASSES - 1),
+                )
+            return acc
+
+        carry = [sb([P, PACK, HALF], F32, "carry%d" % c) for c in range(2)]
+        made = [sb([P, PACK, HALF], F32, "made%d" % c) for c in range(2)]
+        kept = [sb([P, PACK, HALF], F32, "kept%d" % c) for c in range(2)]
+        mixed = [sb([P, PACK, HALF], F32, "mixed%d" % c) for c in range(2)]
+
+        wg_q = quantise_weight(wg_raw, "wg", (0, 1))
+        r_win.append(load_r(2, "wg_raw0"))
+        wh_raw.append(load_weight(wh, 1, "wh_raw1", "wg_raw1"))
+        r_win.append(load_r(3, "wg_bf11"))
+        for t in range(PACK):
+            for c in range(2):
+                acc = product(wg_q, t, c)
+                nc.scalar.activation(
+                    carry[c][:, t, :], acc[:], ACT.Sigmoid, bias=neg_bias[:, t : t + 1], scale=-1.0
+                )
+
+        def keep_part(t, c):
+            cols = HALF // 16
+            nc.vector.tensor_tensor(
+                kept[c][:, t, :],
+                r_win[t][:].indirect(offsets[:, c * cols : (c + 1) * cols]),
+                carry[c][:, t, :],
+                ALU.mult,
+            )
+
+        for t in range(2):
+            for c in range(2):
+                keep_part(t, c)
+
+        keep_part(2, 0)
+        keep_part(2, 1)
+        wh_q = quantise_weight(wh_raw, "wh", (0, 1, 3))
+        for c in range(2):
+            for t in range(PACK):
+                acc = product(wh_q, t, c)
+                nc.scalar.activation(made[c][:, t, :], acc[:], ACT.Tanh)
+
+        y = [sb([P, PACK, w], F32, "y%d" % n) for n, (lo, w) in enumerate(PIECES)]
+        y_rows = out_0.rearrange("(p t) j -> p t j", t=PACK)
+        y_scales = sb([P, J], U8, "y_scales")
+        word_rows = out_1[0].rearrange("p j b -> p (j b)")
+
+        def mix(n, ts):
+            lo, w = PIECES[n]
+            c, j0 = divmod(lo, HALF)
+            nc.vector.scalar_tensor_tensor(
+                mixed[c][:, ts, j0 : j0 + w],
+                carry[c][:, ts, j0 : j0 + w],
+                1.0,
+                made[c][:, ts, j0 : j0 + w],
+                ALU.subtract,
+                ALU.mult,
+            )
+
+        def finish(n, ts):
+            lo, w = PIECES[n]
+            c, j0 = divmod(lo, HALF)
+            nc.vector.tensor_tensor(
+                y[n][:, ts, :], kept[c][:, ts, j0 : j0 + w], mixed[c][:, ts, j0 : j0 + w], ALU.subtract
+            )
+            nc.sync.dma_start(y_rows[:, ts, lo : lo + w], y[n][:, ts, :])
+
+        def round_piece(n):
+            lo, w = PIECES[n]
+            rounded = sb([P, PACK * w], BF16, "y_bf%d" % n)
+            dst = rounded[:].rearrange("p (c i t) -> p c t i", i=4, t=PACK)
+            src = y[n][:].rearrange("p t (c i) -> p c t i", i=4)
+            if n < len(PIECES) - 1:
+                nc.scalar.copy(dst, src)
+            else:
+                nc.vector.tensor_copy(dst, src)
+            return rounded
+
+        def quantise_piece(n, rounded):
+            lo, w = PIECES[n]
+            codes = sb([P, w], U32, "y_codes%d" % n)
+            nc.vector.quantize_mx(
+                out=codes[:].bitcast(FP8X4), scales=y_scales[:, lo : lo + w], in_=rounded[:]
+            )
+            nc.sync.dma_start(word_rows[:, 4 * lo : 4 * (lo + w)].bitcast(I32), codes[:].bitcast(I32))
+
+        low, high, every = slice(0, 2), slice(2, 4), slice(0, 4)
+        keep_part(3, 0)
+        keep_part(3, 1)
+        mix(0, low)
+        mix(0, high)
+        finish(0, low)
+        finish(0, high)
+        rounded0 = round_piece(0)
+        mix(1, every)
+        mix(2, every)
+        finish(1, every)
+        rounded1 = round_piece(1)
+        quantise_piece(0, rounded0)
+        finish(2, every)
+        quantise_piece(1, rounded1)
+        quantise_piece(2, round_piece(2))
+        for q in range(4):
+            queue = nc.scalar if q % 2 else nc.sync
+            queue.dma_start(
+                out_2[0][4 * q : 4 * q + 4, :].bitcast(I32), y_scales[32 * q : 32 * q + 4, :].bitcast(I32)
+            )

@@ -96,8 +96,8 @@ def tile_list_hwayt_tanhP_kernel(
 
         def round_pair(raw, u, on_scalar, name):
             rounded = sb([P, 2 * P * PACK], BF16, name)
-            dst = rounded[:].rearrange("p (t m i) -> p m t i", t=2, i=PACK)
-            src = raw[:].rearrange("p (i m t) -> p m t i", i=PACK, t=PACK)[:, :, 2 * u : 2 * u + 2, :]
+            dst = rounded[:].rearrange("p (t m i) -> p m i t", t=2, i=PACK)
+            src = raw[:].rearrange("p (i m t) -> p m i t", i=PACK, t=PACK)[:, :, :, 2 * u : 2 * u + 2]
             if on_scalar:
                 nc.scalar.copy(dst, src)
             else:
@@ -204,8 +204,8 @@ def tile_list_hwayt_tanhP_kernel(
         def round_piece(n):
             lo, w = PIECES[n]
             rounded = sb([P, PACK * w], BF16, "y_bf%d" % n)
-            dst = rounded[:].rearrange("p (c i t) -> p c t i", i=4, t=PACK)
-            src = y[n][:].rearrange("p t (c i) -> p c t i", i=4)
+            dst = rounded[:].rearrange("p (c i t) -> p c t i", i=2, t=PACK)
+            src = y[n][:].rearrange("p t (c i) -> p c t i", i=2)
             if n < len(PIECES) - 1:
                 nc.scalar.copy(dst, src)
             else:

@@ -96,8 +96,8 @@ def tile_list_hwayt_tanhP_kernel(
 
         def round_pair(raw, u, on_scalar, name):
             rounded = sb([P, 2 * P * PACK], BF16, name)
-            dst = rounded[:].rearrange("p (t m i) -> p m i t", t=2, i=PACK)
-            src = raw[:].rearrange("p (i m t) -> p m i t", i=PACK, t=PACK)[:, :, :, 2 * u : 2 * u + 2]
+            dst = rounded[:].rearrange("p (t m i) -> p m t i", t=2, i=PACK)
+            src = raw[:].rearrange("p (i m t) -> p m t i", i=PACK, t=PACK)[:, :, 2 * u : 2 * u + 2, :]
             if on_scalar:
                 nc.scalar.copy(dst, src)
             else:
@@ -111,70 +111,71 @@ def tile_list_hwayt_tanhP_kernel(
             return codes, scales
 
         def quantise_weight(raw, name, scalar_share):
-            rounded = {
-                (a, u): round_pair(raw[a], u, 2 * a + u in scalar_share, "%s_bf%d%d" % (name, a, u))
-                for a in range(PASSES)
-                for u in range(2)
-            }
-            return {
-                (a, u): quantise_pair(rounded[(a, u)], "%s_q%d%d" % (name, a, u))
-                for a in range(PASSES)
-                for u in range(2)
-            }
+            quantised = {}
+            for u in range(2):
+                rounded = [
+                    round_pair(raw[a], u, (a, u) in scalar_share, "%s_bf%d%d" % (name, a, u))
+                    for a in range(PASSES)
+                ]
+                for a in range(PASSES):
+                    quantised[(a, u)] = quantise_pair(rounded[a], "%s_q%d%d" % (name, a, u))
+            return quantised
 
-        def product(wq, t, c):
-            acc = psum.tile([P, HALF], F32, name="acc")
+        def products(wq, blocks):
+            acc = {block: psum.tile([P, HALF], F32, name="acc") for block in blocks}
             for a in range(PASSES):
-                codes, scales = wq[(a, t // 2)]
-                m = slice(P * (t % 2), P * (t % 2 + 1))
-                lo = 2 * (a * J + c * HALF)
-                nc.tensor.matmul_mx(
-                    out=acc[:],
-                    lhsT=codes[:, m].bitcast(FP8X4),
-                    lhsT_scale=scales[:, m],
-                    rhs=parted[:, lo : lo + 2 * HALF].bitcast(FP4X4),
-                    rhs_scale=planes[:, a * J + c * HALF : a * J + (c + 1) * HALF],
-                    start=(a == 0),
-                    stop=(a == PASSES - 1),
-                )
+                for t, c in blocks:
+                    codes, scales = wq[(a, t // 2)]
+                    m = slice(P * (t % 2), P * (t % 2 + 1))
+                    lo = a * J + c * HALF
+                    nc.tensor.matmul_mx(
+                        out=acc[(t, c)][:],
+                        lhsT=codes[:, m].bitcast(FP8X4),
+                        lhsT_scale=scales[:, m],
+                        rhs=parted[:, 2 * lo : 2 * (lo + HALF)].bitcast(FP4X4),
+                        rhs_scale=planes[:, lo : lo + HALF],
+                        start=(a == 0),
+                        stop=(a == PASSES - 1),
+                    )
             return acc
 
-        carry = [sb([P, PACK, HALF], F32, "carry%d" % c) for c in range(2)]
-        made = [sb([P, PACK, HALF], F32, "made%d" % c) for c in range(2)]
-        kept = [sb([P, PACK, HALF], F32, "kept%d" % c) for c in range(2)]
-        mixed = [sb([P, PACK, HALF], F32, "mixed%d" % c) for c in range(2)]
+        carry = sb([P, PACK, J], F32, "carry")
+        made = sb([P, PACK, J], F32, "made")
+        kept = sb([P, PACK, J], F32, "kept")
+        mixed = sb([P, PACK, J], F32, "mixed")
 
-        wg_q = quantise_weight(wg_raw, "wg", (0, 1))
+        wg_q = quantise_weight(wg_raw, "wg", ((0, 0), (0, 1)))
         r_win.append(load_r(2, "wg_raw0"))
         wh_raw.append(load_weight(wh, 1, "wh_raw1", "wg_raw1"))
         r_win.append(load_r(3, "wg_bf11"))
         for t in range(PACK):
             for c in range(2):
-                acc = product(wg_q, t, c)
+                acc = products(wg_q, [(t, c)])
                 nc.scalar.activation(
-                    carry[c][:, t, :], acc[:], ACT.Sigmoid, bias=neg_bias[:, t : t + 1], scale=-1.0
+                    carry[:, t, c * HALF : (c + 1) * HALF],
+                    acc[(t, c)][:],
+                    ACT.Sigmoid,
+                    bias=neg_bias[:, t : t + 1],
+                    scale=-1.0,
                 )
 
-        def keep_part(t, c):
-            cols = HALF // 16
+        def keep_part(t, lo, w):
             nc.vector.tensor_tensor(
-                kept[c][:, t, :],
-                r_win[t][:].indirect(offsets[:, c * cols : (c + 1) * cols]),
-                carry[c][:, t, :],
+                kept[:, t, lo : lo + w],
+                r_win[t][:].indirect(offsets[:, lo // 16 : (lo + w) // 16]),
+                carry[:, t, lo : lo + w],
                 ALU.mult,
             )
 
-        for t in range(2):
-            for c in range(2):
-                keep_part(t, c)
-
-        keep_part(2, 0)
-        keep_part(2, 1)
-        wh_q = quantise_weight(wh_raw, "wh", (0, 1, 3))
-        for c in range(2):
-            for t in range(PACK):
-                acc = product(wh_q, t, c)
-                nc.scalar.activation(made[c][:, t, :], acc[:], ACT.Tanh)
+        keep_part(0, 0, HALF)
+        keep_part(0, HALF, HALF)
+        keep_part(1, 0, J)
+        keep_part(2, 0, J)
+        wh_q = quantise_weight(wh_raw, "wh", ((0, 0), (0, 1), (1, 1)))
+        blocks = [(t, c) for c in range(2) for t in range(PACK)]
+        acc = products(wh_q, blocks)
+        for t, c in blocks:
+            nc.scalar.activation(made[:, t, c * HALF : (c + 1) * HALF], acc[(t, c)][:], ACT.Tanh)
 
         y = [sb([P, PACK, w], F32, "y%d" % n) for n, (lo, w) in enumerate(PIECES)]
         y_rows = out_0.rearrange("(p t) j -> p t j", t=PACK)
@@ -183,21 +184,19 @@ def tile_list_hwayt_tanhP_kernel(
 
         def mix(n, ts):
             lo, w = PIECES[n]
-            c, j0 = divmod(lo, HALF)
             nc.vector.scalar_tensor_tensor(
-                mixed[c][:, ts, j0 : j0 + w],
-                carry[c][:, ts, j0 : j0 + w],
+                mixed[:, ts, lo : lo + w],
+                carry[:, ts, lo : lo + w],
                 1.0,
-                made[c][:, ts, j0 : j0 + w],
+                made[:, ts, lo : lo + w],
                 ALU.subtract,
                 ALU.mult,
             )
 
         def finish(n, ts):
             lo, w = PIECES[n]
-            c, j0 = divmod(lo, HALF)
             nc.vector.tensor_tensor(
-                y[n][:, ts, :], kept[c][:, ts, j0 : j0 + w], mixed[c][:, ts, j0 : j0 + w], ALU.subtract
+                y[n][:, ts, :], kept[:, ts, lo : lo + w], mixed[:, ts, lo : lo + w], ALU.subtract
             )
             nc.sync.dma_start(y_rows[:, ts, lo : lo + w], y[n][:, ts, :])
 
@@ -221,8 +220,7 @@ def tile_list_hwayt_tanhP_kernel(
             nc.sync.dma_start(word_rows[:, 4 * lo : 4 * (lo + w)].bitcast(I32), codes[:].bitcast(I32))
 
         low, high, every = slice(0, 2), slice(2, 4), slice(0, 4)
-        keep_part(3, 0)
-        keep_part(3, 1)
+        keep_part(3, 0, J)
         mix(0, low)
         mix(0, high)
         finish(0, low)

@@ -29,7 +29,8 @@ def tile_list_hwayt_tanhP_kernel(
     nc = tc.nc
     with ExitStack() as ctx:
         keep = ctx.enter_context(tc.tile_pool(name="keep", bufs=1))
-        psum = ctx.enter_context(tc.psum_pool(name="psum", bufs=8))
+        gate_banks = ctx.enter_context(tc.psum_pool(name="gate_banks", bufs=2))
+        made_banks = ctx.enter_context(tc.psum_pool(name="made_banks", bufs=6))
 
         def sb(shape, dtype, name, tag=None):
             return keep.tile(shape, dtype, name=name, tag=tag or name, align_bytes=64)
@@ -86,18 +87,18 @@ def tile_list_hwayt_tanhP_kernel(
 
         picked = sb([P, J], U32, "picked")
         nc.vector.tensor_copy(picked[:], word_win[:].indirect(offsets[:]))
-        r_win.append(load_r(1, "word_win"))
+        wh_raw = [load_weight(wh, 0, "wh_raw0", "word_win")]
         parted = sb([P, PASSES * 2 * J], U8, "parted")
         nc.vector.tensor_copy(
             parted[:].bitcast(U16).rearrange("p (d j) -> p d j", d=PASSES),
             picked[:].bitcast(U16).rearrange("p (j d) -> p d j", d=PASSES),
         )
-        wh_raw = [load_weight(wh, 0, "wh_raw0", "picked")]
+        r_win.append(load_r(1, "picked"))
 
         def round_pair(raw, u, on_scalar, name):
             rounded = sb([P, 2 * P * PACK], BF16, name)
-            dst = rounded[:].rearrange("p (t m i) -> p m t i", t=2, i=PACK)
-            src = raw[:].rearrange("p (i m t) -> p m t i", i=PACK, t=PACK)[:, :, 2 * u : 2 * u + 2, :]
+            dst = rounded[:].rearrange("p (t m i) -> p m i t", t=2, i=PACK)
+            src = raw[:].rearrange("p (i m t) -> p m i t", i=PACK, t=PACK)[:, :, :, 2 * u : 2 * u + 2]
             if on_scalar:
                 nc.scalar.copy(dst, src)
             else:
@@ -121,8 +122,8 @@ def tile_list_hwayt_tanhP_kernel(
                     quantised[(a, u)] = quantise_pair(rounded[a], "%s_q%d%d" % (name, a, u))
             return quantised
 
-        def products(wq, blocks):
-            acc = {block: psum.tile([P, HALF], F32, name="acc") for block in blocks}
+        def products(banks, wq, blocks):
+            acc = {block: banks.tile([P, HALF], F32, name="acc") for block in blocks}
             for a in range(PASSES):
                 for t, c in blocks:
                     codes, scales = wq[(a, t // 2)]
@@ -144,13 +145,13 @@ def tile_list_hwayt_tanhP_kernel(
         kept = sb([P, PACK, J], F32, "kept")
         mixed = sb([P, PACK, J], F32, "mixed")
 
-        wg_q = quantise_weight(wg_raw, "wg", ((0, 0), (0, 1)))
+        wg_q = quantise_weight(wg_raw, "wg", ((0, 0), (0, 1), (1, 1)))
         r_win.append(load_r(2, "wg_raw0"))
         wh_raw.append(load_weight(wh, 1, "wh_raw1", "wg_raw1"))
         r_win.append(load_r(3, "wg_bf11"))
         for t in range(PACK):
             for c in range(2):
-                acc = products(wg_q, [(t, c)])
+                acc = products(gate_banks, wg_q, [(t, c)])
                 nc.scalar.activation(
                     carry[:, t, c * HALF : (c + 1) * HALF],
                     acc[(t, c)][:],
@@ -171,10 +172,10 @@ def tile_list_hwayt_tanhP_kernel(
         keep_part(0, HALF, HALF)
         keep_part(1, 0, J)
         keep_part(2, 0, J)
-        wh_q = quantise_weight(wh_raw, "wh", ((0, 0), (0, 1), (1, 1)))
+        wh_q = quantise_weight(wh_raw, "wh", ((1, 0), (1, 1)))
         blocks = [(t, c) for c in range(2) for t in range(PACK)]
-        acc = products(wh_q, blocks)
         for t, c in blocks:
+            acc = products(made_banks, wh_q, [(t, c)])
             nc.scalar.activation(made[:, t, c * HALF : (c + 1) * HALF], acc[(t, c)][:], ACT.Tanh)
 
         y = [sb([P, PACK, w], F32, "y%d" % n) for n, (lo, w) in enumerate(PIECES)]
@@ -220,7 +221,8 @@ def tile_list_hwayt_tanhP_kernel(
             nc.sync.dma_start(word_rows[:, 4 * lo : 4 * (lo + w)].bitcast(I32), codes[:].bitcast(I32))
 
         low, high, every = slice(0, 2), slice(2, 4), slice(0, 4)
-        keep_part(3, 0, J)
+        keep_part(3, 0, HALF)
+        keep_part(3, HALF, HALF)
         mix(0, low)
         mix(0, high)
         finish(0, low)

@@ -1,6 +1,7 @@
 from contextlib import ExitStack
 
 import concourse.mybir as mybir
+from concourse.masks import make_identity
 
 K, N, T, J = 1024, 512, 2048, 1024
 FLOPS = 2 * 2 * K * N * J
@@ -20,7 +21,8 @@ P = 128
 PACK = 4
 PASSES = 2
 HALF = 512
-PIECES = ((0, 512), (512, 256), (768, 256))
+PIECE = 256
+ON_TENSOR = ((0, 0), (0, 1), (1, 0), (1, 1))
 
 
 def tile_list_hwayt_tanhP_kernel(
@@ -30,7 +32,8 @@ def tile_list_hwayt_tanhP_kernel(
     with ExitStack() as ctx:
         keep = ctx.enter_context(tc.tile_pool(name="keep", bufs=1))
         gate_banks = ctx.enter_context(tc.psum_pool(name="gate_banks", bufs=2))
-        made_banks = ctx.enter_context(tc.psum_pool(name="made_banks", bufs=6))
+        made_banks = ctx.enter_context(tc.psum_pool(name="made_banks", bufs=4))
+        sum_banks = ctx.enter_context(tc.psum_pool(name="sum_banks", bufs=2))
 
         def sb(shape, dtype, name, tag=None):
             return keep.tile(shape, dtype, name=name, tag=tag or name, align_bytes=64)
@@ -39,14 +42,18 @@ def tile_list_hwayt_tanhP_kernel(
         nc.sync.dma_start(offsets[:], offs)
 
         scale_win = sb([P, T], U8, "scale_win")
+        nc.sync.dma_start(scale_win[12:28, :].bitcast(I32), tab_scales[1].bitcast(I32))
         for q in range(4):
-            nc.vector.memset(scale_win[32 * q : 32 * q + 24, :].bitcast(I32), 0)
+            nc.vector.memset(scale_win[32 * q : 32 * q + (28 if q else 12), :].bitcast(I32), 0)
             nc.sync.dma_start(
-                scale_win[32 * q + 24 : 32 * q + 32, :].bitcast(I32),
-                tab_scales[:, 4 * q : 4 * q + 4, :].bitcast(I32),
+                scale_win[32 * q + 28 : 32 * q + 32, :].bitcast(I32),
+                tab_scales[0, 4 * q : 4 * q + 4, :].bitcast(I32),
             )
         planes = sb([P, PASSES * J], U8, "planes")
         nc.gpsimd.memset(planes[:].bitcast(I32), 0)
+
+        identity = sb([P, P], F32, "identity")
+        make_identity(nc, identity[:])
 
         word_win = sb([P, T], U32, "word_win")
         nc.sync.dma_start(
@@ -70,30 +77,28 @@ def tile_list_hwayt_tanhP_kernel(
         wg_raw = [load_weight(wg, a, "wg_raw%d" % a) for a in range(PASSES)]
         bias = sb([P, PACK], F32, "bias")
         nc.scalar.dma_start(bias[:], bg.rearrange("(p t) -> p t", t=PACK))
-
         neg_bias = sb([P, PACK], F32, "neg_bias")
-        nc.gpsimd.tensor_scalar(neg_bias[:], bias[:], -1.0, 0.0, ALU.mult, ALU.add)
-        warm = sb([P, 1], F32, "warm")
-        nc.scalar.activation(warm[:], bias[:, 0:1], ACT.Sigmoid)
+        nc.scalar.mul(neg_bias[:], bias[:], -1.0)
 
         picked_scales = sb([P, J], U8, "picked_scales")
         nc.vector.tensor_copy(picked_scales[:], scale_win[:].indirect(offsets[:]))
-        for a in range(PASSES):
+        nc.sync.dma_start(planes[0:100, 0:J].bitcast(I32), picked_scales[28:128, :].bitcast(I32))
+        for q in range(4):
             nc.sync.dma_start(
-                planes[0:100, a * J : (a + 1) * J].bitcast(I32),
-                picked_scales[24 + 4 * a : 124 + 4 * a, :].bitcast(I32),
+                planes[32 * q : 32 * q + 4, J : 2 * J].bitcast(I32),
+                picked_scales[12 + 4 * q : 16 + 4 * q, :].bitcast(I32),
             )
-        r_win = [load_r(0, "scale_win")]
 
+        wh_raw = [load_weight(wh, 0, "wh_raw0", "scale_win")]
         picked = sb([P, J], U32, "picked")
         nc.vector.tensor_copy(picked[:], word_win[:].indirect(offsets[:]))
-        wh_raw = [load_weight(wh, 0, "wh_raw0", "word_win")]
+        r_win = [load_r(0, "word_win")]
         parted = sb([P, PASSES * 2 * J], U8, "parted")
         nc.vector.tensor_copy(
             parted[:].bitcast(U16).rearrange("p (d j) -> p d j", d=PASSES),
             picked[:].bitcast(U16).rearrange("p (j d) -> p d j", d=PASSES),
         )
-        r_win.append(load_r(1, "picked"))
+        wh_raw.append(load_weight(wh, 1, "wh_raw1", "picked"))
 
         def round_pair(raw, u, on_scalar, name):
             rounded = sb([P, 2 * P * PACK], BF16, name)
@@ -111,131 +116,178 @@ def tile_list_hwayt_tanhP_kernel(
             nc.vector.quantize_mx(out=codes[:].bitcast(FP8X4), scales=scales[:], in_=rounded[:])
             return codes, scales
 
-        def quantise_weight(raw, name, scalar_share):
-            quantised = {}
-            for u in range(2):
-                rounded = [
-                    round_pair(raw[a], u, (a, u) in scalar_share, "%s_bf%d%d" % (name, a, u))
-                    for a in range(PASSES)
-                ]
-                for a in range(PASSES):
-                    quantised[(a, u)] = quantise_pair(rounded[a], "%s_q%d%d" % (name, a, u))
-            return quantised
-
-        def products(banks, wq, blocks):
-            acc = {block: banks.tile([P, HALF], F32, name="acc") for block in blocks}
+        def product(banks, wq, t, c):
+            acc = banks.tile([P, HALF], F32, name="acc")
             for a in range(PASSES):
-                for t, c in blocks:
-                    codes, scales = wq[(a, t // 2)]
-                    m = slice(P * (t % 2), P * (t % 2 + 1))
-                    lo = a * J + c * HALF
-                    nc.tensor.matmul_mx(
-                        out=acc[(t, c)][:],
-                        lhsT=codes[:, m].bitcast(FP8X4),
-                        lhsT_scale=scales[:, m],
-                        rhs=parted[:, 2 * lo : 2 * (lo + HALF)].bitcast(FP4X4),
-                        rhs_scale=planes[:, lo : lo + HALF],
-                        start=(a == 0),
-                        stop=(a == PASSES - 1),
-                    )
+                codes, scales = wq[(a, t // 2)]
+                m = slice(P * (t % 2), P * (t % 2 + 1))
+                lo = a * J + c * HALF
+                nc.tensor.matmul_mx(
+                    out=acc[:],
+                    lhsT=codes[:, m].bitcast(FP8X4),
+                    lhsT_scale=scales[:, m],
+                    rhs=parted[:, 2 * lo : 2 * (lo + HALF)].bitcast(FP4X4),
+                    rhs_scale=planes[:, lo : lo + HALF],
+                    start=(a == 0),
+                    stop=(a == PASSES - 1),
+                )
             return acc
 
-        carry = sb([P, PACK, J], F32, "carry")
-        made = sb([P, PACK, J], F32, "made")
+        carry = [sb([P, J], F32, "carry%d" % t) for t in range(PACK - 1)]
+        neg_made = sb([P, PACK, J], F32, "neg_made")
         kept = sb([P, PACK, J], F32, "kept")
         mixed = sb([P, PACK, J], F32, "mixed")
 
-        wg_q = quantise_weight(wg_raw, "wg", ((0, 0), (0, 1), (1, 1)))
-        r_win.append(load_r(2, "wg_raw0"))
-        wh_raw.append(load_weight(wh, 1, "wh_raw1", "wg_raw1"))
+        wg_bf = {(0, u): round_pair(wg_raw[0], u, True, "wg_bf0%d" % u) for u in range(2)}
+        r_win.append(load_r(1, "wg_raw0"))
+        wg_q = {(0, 0): quantise_pair(wg_bf[(0, 0)], "wg_q00")}
+        wg_bf[(1, 0)] = round_pair(wg_raw[1], 0, False, "wg_bf10")
+        wg_q[(0, 1)] = quantise_pair(wg_bf[(0, 1)], "wg_q01")
+        wg_q[(1, 0)] = quantise_pair(wg_bf[(1, 0)], "wg_q10")
+        wg_bf[(1, 1)] = round_pair(wg_raw[1], 1, True, "wg_bf11")
+        r_win.append(load_r(2, "wg_raw1"))
+        wg_q[(1, 1)] = quantise_pair(wg_bf[(1, 1)], "wg_q11")
         r_win.append(load_r(3, "wg_bf11"))
-        for t in range(PACK):
+
+        def gate(t):
             for c in range(2):
-                acc = products(gate_banks, wg_q, [(t, c)])
+                acc = product(gate_banks, wg_q, t, c)
                 nc.scalar.activation(
-                    carry[:, t, c * HALF : (c + 1) * HALF],
-                    acc[(t, c)][:],
+                    carry[t][:, c * HALF : (c + 1) * HALF],
+                    acc[:],
                     ACT.Sigmoid,
                     bias=neg_bias[:, t : t + 1],
                     scale=-1.0,
                 )
 
-        def keep_part(t, lo, w):
+        def pick(t, lo, w):
             nc.vector.tensor_tensor(
                 kept[:, t, lo : lo + w],
                 r_win[t][:].indirect(offsets[:, lo // 16 : (lo + w) // 16]),
-                carry[:, t, lo : lo + w],
+                carry[t][:, lo : lo + w],
                 ALU.mult,
             )
 
-        keep_part(0, 0, HALF)
-        keep_part(0, HALF, HALF)
-        keep_part(1, 0, J)
-        keep_part(2, 0, J)
-        wh_q = quantise_weight(wh_raw, "wh", ((1, 0), (1, 1)))
-        blocks = [(t, c) for c in range(2) for t in range(PACK)]
-        for t, c in blocks:
-            acc = products(made_banks, wh_q, [(t, c)])
-            nc.scalar.activation(made[:, t, c * HALF : (c + 1) * HALF], acc[(t, c)][:], ACT.Tanh)
+        gate(0)
+        wh_q = {}
+        for a in range(PASSES):
+            if a == 1:
+                pick(0, 0, HALF)
+                pick(0, HALF, HALF)
+            wh_bf = [round_pair(wh_raw[a], u, (a, u) == (1, 1), "wh_bf%d%d" % (a, u)) for u in range(2)]
+            for u in range(2):
+                wh_q[(a, u)] = quantise_pair(wh_bf[u], "wh_q%d%d" % (a, u))
+        gate(1)
+        gate(2)
+        carry.append(sb([P, J], F32, "carry3", "picked"))
 
-        y = [sb([P, PACK, w], F32, "y%d" % n) for n, (lo, w) in enumerate(PIECES)]
+        for t in range(PACK):
+            if t == 2:
+                gate(3)
+            for c in range(2):
+                acc = product(made_banks, wh_q, t, c)
+                nc.scalar.activation(
+                    neg_made[:, t, c * HALF : (c + 1) * HALF], acc[:], ACT.Tanh, scale=-1.0
+                )
+
+        y = sb([P, PACK, J], F32, "y")
         y_rows = out_0.rearrange("(p t) j -> p t j", t=PACK)
         y_scales = sb([P, J], U8, "y_scales")
         word_rows = out_1[0].rearrange("p j b -> p (j b)")
 
-        def mix(n, ts):
-            lo, w = PIECES[n]
+        def mix(t, lo, w):
             nc.vector.scalar_tensor_tensor(
-                mixed[:, ts, lo : lo + w],
-                carry[:, ts, lo : lo + w],
+                mixed[:, t, lo : lo + w],
+                carry[t][:, lo : lo + w],
                 1.0,
-                made[:, ts, lo : lo + w],
+                neg_made[:, t, lo : lo + w],
                 ALU.subtract,
                 ALU.mult,
             )
 
-        def finish(n, ts):
-            lo, w = PIECES[n]
+        def finish(t, lo, w):
             nc.vector.tensor_tensor(
-                y[n][:, ts, :], kept[:, ts, lo : lo + w], mixed[:, ts, lo : lo + w], ALU.subtract
+                y[:, t, lo : lo + w], kept[:, t, lo : lo + w], mixed[:, t, lo : lo + w], ALU.add
             )
-            nc.sync.dma_start(y_rows[:, ts, lo : lo + w], y[n][:, ts, :])
 
-        def round_piece(n):
-            lo, w = PIECES[n]
-            rounded = sb([P, PACK * w], BF16, "y_bf%d" % n)
+        def finish_on_tensor(t, c):
+            summed = (gate_banks if t else sum_banks).tile([P, HALF], F32, name="acc")
+            for b in range(PACK):
+                cols = slice(c * HALF + b * P, c * HALF + (b + 1) * P)
+                for n, term in enumerate((kept, mixed)):
+                    nc.tensor.matmul(
+                        summed[:, b * P : (b + 1) * P],
+                        lhsT=term[:, t, cols],
+                        rhs=identity[:],
+                        is_transpose=True,
+                        start=(n == 0),
+                        stop=(n == 1),
+                    )
+            turned = sb([P, HALF], F32, "turned%d%d" % (t, c))
+            nc.scalar.copy(turned[:], summed[:])
+            back = made_banks.tile([P, HALF], F32, name="acc")
+            for b in range(PACK):
+                nc.tensor.transpose(back[:, b * P : (b + 1) * P], turned[:, b * P : (b + 1) * P], identity[:])
+            nc.scalar.copy(y[:, t, c * HALF : (c + 1) * HALF], back[:])
+
+        def store(t, lo, w):
+            nc.sync.dma_start(y_rows[:, t, lo : lo + w], y[:, t, lo : lo + w])
+
+        def round_part(lo, w, on_scalar):
+            rounded = sb([P, PACK * w], BF16, "y_bf%d" % lo)
             dst = rounded[:].rearrange("p (c i t) -> p c t i", i=2, t=PACK)
-            src = y[n][:].rearrange("p t (c i) -> p c t i", i=2)
-            if n < len(PIECES) - 1:
+            src = y[:, :, lo : lo + w].rearrange("p t (c i) -> p c t i", i=2)
+            if on_scalar:
                 nc.scalar.copy(dst, src)
             else:
                 nc.vector.tensor_copy(dst, src)
             return rounded
 
-        def quantise_piece(n, rounded):
-            lo, w = PIECES[n]
-            codes = sb([P, w], U32, "y_codes%d" % n)
+        def quantise_part(lo, w, rounded):
+            codes = sb([P, w], U32, "y_codes%d" % lo)
             nc.vector.quantize_mx(
                 out=codes[:].bitcast(FP8X4), scales=y_scales[:, lo : lo + w], in_=rounded[:]
             )
             nc.sync.dma_start(word_rows[:, 4 * lo : 4 * (lo + w)].bitcast(I32), codes[:].bitcast(I32))
 
-        low, high, every = slice(0, 2), slice(2, 4), slice(0, 4)
-        keep_part(3, 0, HALF)
-        keep_part(3, HALF, HALF)
-        mix(0, low)
-        mix(0, high)
-        finish(0, low)
-        finish(0, high)
-        rounded0 = round_piece(0)
-        mix(1, every)
-        mix(2, every)
-        finish(1, every)
-        rounded1 = round_piece(1)
-        quantise_piece(0, rounded0)
-        finish(2, every)
-        quantise_piece(1, rounded1)
-        quantise_piece(2, round_piece(2))
+        for t in range(PACK - 1):
+            if t > 0:
+                for c in range(2):
+                    pick(t, c * HALF, HALF)
+            for c in range(2):
+                mix(t, c * HALF, HALF)
+            for c in range(2):
+                if (t, c) in ON_TENSOR:
+                    finish_on_tensor(t, c)
+                else:
+                    finish(t, c * HALF, HALF)
+                store(t, c * HALF, HALF)
+
+        last = PACK - 1
+        mix(last, 0, J)
+        rounded = {}
+
+        def close(n):
+            finish(last, n * PIECE, PIECE)
+            store(last, n * PIECE, PIECE)
+            if n < 3:
+                rounded[n] = round_part(n * PIECE, PIECE, True)
+
+        pick(last, 0, PIECE)
+        pick(last, PIECE, PIECE)
+        close(0)
+        pick(last, 2 * PIECE, PIECE)
+        close(1)
+        pick(last, 3 * PIECE, PIECE)
+        close(2)
+        quantise_part(0, PIECE, rounded[0])
+        close(3)
+        quantise_part(PIECE, PIECE, rounded[1])
+        high = round_part(896, 128, False)
+        low = round_part(768, 128, True)
+        quantise_part(2 * PIECE, PIECE, rounded[2])
+        quantise_part(896, 128, high)
+        quantise_part(768, 128, low)
         for q in range(4):
             queue = nc.scalar if q % 2 else nc.sync
             queue.dma_start(

@@ -22,7 +22,6 @@ PACK = 4
 PASSES = 2
 HALF = 512
 PIECE = 256
-ON_TENSOR = ((0, 0), (0, 1), (1, 0), (1, 1))
 
 
 def tile_list_hwayt_tanhP_kernel(
@@ -31,9 +30,10 @@ def tile_list_hwayt_tanhP_kernel(
     nc = tc.nc
     with ExitStack() as ctx:
         keep = ctx.enter_context(tc.tile_pool(name="keep", bufs=1))
-        gate_banks = ctx.enter_context(tc.psum_pool(name="gate_banks", bufs=2))
-        made_banks = ctx.enter_context(tc.psum_pool(name="made_banks", bufs=4))
-        sum_banks = ctx.enter_context(tc.psum_pool(name="sum_banks", bufs=2))
+        psum = ctx.enter_context(tc.psum_pool(name="psum", bufs=1))
+
+        def bank(b):
+            return psum.tile([P, HALF], F32, name="bank%d" % b, tag="bank%d" % b)
 
         def sb(shape, dtype, name, tag=None):
             return keep.tile(shape, dtype, name=name, tag=tag or name, align_bytes=64)
@@ -92,13 +92,13 @@ def tile_list_hwayt_tanhP_kernel(
         wh_raw = [load_weight(wh, 0, "wh_raw0", "scale_win")]
         picked = sb([P, J], U32, "picked")
         nc.vector.tensor_copy(picked[:], word_win[:].indirect(offsets[:]))
-        r_win = [load_r(0, "word_win")]
+        wh_raw.append(load_weight(wh, 1, "wh_raw1", "word_win"))
         parted = sb([P, PASSES * 2 * J], U8, "parted")
         nc.vector.tensor_copy(
             parted[:].bitcast(U16).rearrange("p (d j) -> p d j", d=PASSES),
             picked[:].bitcast(U16).rearrange("p (j d) -> p d j", d=PASSES),
         )
-        wh_raw.append(load_weight(wh, 1, "wh_raw1", "picked"))
+        r_win = [load_r(0, "picked")]
 
         def round_pair(raw, u, on_scalar, name):
             rounded = sb([P, 2 * P * PACK], BF16, name)
@@ -116,9 +116,9 @@ def tile_list_hwayt_tanhP_kernel(
             nc.vector.quantize_mx(out=codes[:].bitcast(FP8X4), scales=scales[:], in_=rounded[:])
             return codes, scales
 
-        def product(banks, wq, t, c):
-            acc = banks.tile([P, HALF], F32, name="acc")
-            for a in range(PASSES):
+        def product(b, wq, t, c, order=(0, 1)):
+            acc = bank(b)
+            for a in order:
                 codes, scales = wq[(a, t // 2)]
                 m = slice(P * (t % 2), P * (t % 2 + 1))
                 lo = a * J + c * HALF
@@ -128,15 +128,19 @@ def tile_list_hwayt_tanhP_kernel(
                     lhsT_scale=scales[:, m],
                     rhs=parted[:, 2 * lo : 2 * (lo + HALF)].bitcast(FP4X4),
                     rhs_scale=planes[:, lo : lo + HALF],
-                    start=(a == 0),
-                    stop=(a == PASSES - 1),
+                    start=(a == order[0]),
+                    stop=(a == order[1]),
                 )
             return acc
 
-        carry = [sb([P, J], F32, "carry%d" % t) for t in range(PACK - 1)]
-        neg_made = sb([P, PACK, J], F32, "neg_made")
-        kept = sb([P, PACK, J], F32, "kept")
-        mixed = sb([P, PACK, J], F32, "mixed")
+        def half(name, t, c, tag=None):
+            return sb([P, HALF], F32, "%s%d%d" % (name, t, c), tag)
+
+        blocks = [(t, c) for t in range(PACK) for c in range(2)]
+        carry = {b: half("carry", *b) for b in blocks}
+        neg_made = [sb([P, J], F32, "neg_made%d" % t) for t in range(PACK)]
+        kept = {(t, c): half("kept", t, c) for t in range(PACK) for c in range(2) if (t, c) not in [(1, 1), (2, 1)]}
+        mixed = {b: half("mixed", *b) for b in blocks if b not in [(1, 1), (2, 1)]}
 
         wg_bf = {(0, u): round_pair(wg_raw[0], u, True, "wg_bf0%d" % u) for u in range(2)}
         r_win.append(load_r(1, "wg_raw0"))
@@ -144,99 +148,94 @@ def tile_list_hwayt_tanhP_kernel(
         wg_bf[(1, 0)] = round_pair(wg_raw[1], 0, False, "wg_bf10")
         wg_q[(0, 1)] = quantise_pair(wg_bf[(0, 1)], "wg_q01")
         wg_q[(1, 0)] = quantise_pair(wg_bf[(1, 0)], "wg_q10")
-        wg_bf[(1, 1)] = round_pair(wg_raw[1], 1, True, "wg_bf11")
+        wg_bf[(1, 1)] = round_pair(wg_raw[1], 1, False, "wg_bf11")
         r_win.append(load_r(2, "wg_raw1"))
         wg_q[(1, 1)] = quantise_pair(wg_bf[(1, 1)], "wg_q11")
         r_win.append(load_r(3, "wg_bf11"))
 
         def gate(t):
             for c in range(2):
-                acc = product(gate_banks, wg_q, t, c)
+                acc = product((2 * t + c) % 4, wg_q, t, c, (1, 0) if t else (0, 1))
                 nc.scalar.activation(
-                    carry[t][:, c * HALF : (c + 1) * HALF],
-                    acc[:],
-                    ACT.Sigmoid,
-                    bias=neg_bias[:, t : t + 1],
-                    scale=-1.0,
+                    carry[(t, c)][:], acc[:], ACT.Sigmoid, bias=neg_bias[:, t : t + 1], scale=-1.0
                 )
 
-        def pick(t, lo, w):
+        def pick(t, c, lo=0, w=HALF):
+            at = c * HALF + lo
             nc.vector.tensor_tensor(
-                kept[:, t, lo : lo + w],
-                r_win[t][:].indirect(offsets[:, lo // 16 : (lo + w) // 16]),
-                carry[t][:, lo : lo + w],
+                kept[(t, c)][:, lo : lo + w],
+                r_win[t][:].indirect(offsets[:, at // 16 : (at + w) // 16]),
+                carry[(t, c)][:, lo : lo + w],
                 ALU.mult,
             )
 
         gate(0)
+        gate(1)
         wh_q = {}
         for a in range(PASSES):
-            if a == 1:
-                pick(0, 0, HALF)
-                pick(0, HALF, HALF)
-            wh_bf = [round_pair(wh_raw[a], u, (a, u) == (1, 1), "wh_bf%d%d" % (a, u)) for u in range(2)]
+            wh_bf = [round_pair(wh_raw[a], u, False, "wh_bf%d%d" % (a, u)) for u in range(2)]
             for u in range(2):
                 wh_q[(a, u)] = quantise_pair(wh_bf[u], "wh_q%d%d" % (a, u))
-        gate(1)
         gate(2)
-        carry.append(sb([P, J], F32, "carry3", "picked"))
+        gate(3)
 
-        for t in range(PACK):
-            if t == 2:
-                gate(3)
-            for c in range(2):
-                acc = product(made_banks, wh_q, t, c)
-                nc.scalar.activation(
-                    neg_made[:, t, c * HALF : (c + 1) * HALF], acc[:], ACT.Tanh, scale=-1.0
-                )
+        def make(t, c, b):
+            acc = product(b, wh_q, t, c)
+            nc.scalar.activation(neg_made[t][:, c * HALF : (c + 1) * HALF], acc[:], ACT.Tanh, scale=-1.0)
 
-        y = sb([P, PACK, J], F32, "y")
+        for n, (t, c) in enumerate(blocks[:4]):
+            make(t, c, 4 + n)
+        make(2, 0, 6)
+
+        y = [sb([P, PACK, HALF], F32, "y%d" % c) for c in range(2)]
         y_rows = out_0.rearrange("(p t) j -> p t j", t=PACK)
         y_scales = sb([P, J], U8, "y_scales")
         word_rows = out_1[0].rearrange("p j b -> p (j b)")
 
-        def mix(t, lo, w):
+        def mix(t, c):
+            cols = slice(c * HALF, (c + 1) * HALF)
             nc.vector.scalar_tensor_tensor(
-                mixed[:, t, lo : lo + w],
-                carry[t][:, lo : lo + w],
-                1.0,
-                neg_made[:, t, lo : lo + w],
-                ALU.subtract,
-                ALU.mult,
+                mixed[(t, c)][:, :], carry[(t, c)][:], 1.0, neg_made[t][:, cols], ALU.subtract, ALU.mult
             )
 
-        def finish(t, lo, w):
+        def finish(t, c, lo=0, w=HALF):
             nc.vector.tensor_tensor(
-                y[:, t, lo : lo + w], kept[:, t, lo : lo + w], mixed[:, t, lo : lo + w], ALU.add
+                y[c][:, t, lo : lo + w], kept[(t, c)][:, lo : lo + w], mixed[(t, c)][:, lo : lo + w], ALU.add
             )
 
-        def finish_on_tensor(t, c):
-            summed = (gate_banks if t else sum_banks).tile([P, HALF], F32, name="acc")
-            for b in range(PACK):
-                cols = slice(c * HALF + b * P, c * HALF + (b + 1) * P)
-                for n, term in enumerate((kept, mixed)):
+        def store(t, c):
+            nc.sync.dma_start(y_rows[:, t, c * HALF : (c + 1) * HALF], y[c][:, t, :])
+
+        turned = {}
+
+        def sum_turned(t, c, b):
+            summed = bank(b)
+            for k in range(PACK):
+                cols = slice(k * P, (k + 1) * P)
+                for n, term in enumerate((kept[(t, c)], mixed[(t, c)])):
                     nc.tensor.matmul(
-                        summed[:, b * P : (b + 1) * P],
-                        lhsT=term[:, t, cols],
+                        summed[:, k * P : (k + 1) * P],
+                        lhsT=term[:, cols],
                         rhs=identity[:],
                         is_transpose=True,
                         start=(n == 0),
                         stop=(n == 1),
                     )
-            turned = sb([P, HALF], F32, "turned%d%d" % (t, c))
-            nc.scalar.copy(turned[:], summed[:])
-            back = made_banks.tile([P, HALF], F32, name="acc")
-            for b in range(PACK):
-                nc.tensor.transpose(back[:, b * P : (b + 1) * P], turned[:, b * P : (b + 1) * P], identity[:])
-            nc.scalar.copy(y[:, t, c * HALF : (c + 1) * HALF], back[:])
+            turned[(t, c)] = half("turned", t, c)
+            nc.scalar.copy(turned[(t, c)][:], summed[:])
 
-        def store(t, lo, w):
-            nc.sync.dma_start(y_rows[:, t, lo : lo + w], y[:, t, lo : lo + w])
+        def turn_back(t, c, b):
+            back = bank(b)
+            for k in range(PACK):
+                cols = slice(k * P, (k + 1) * P)
+                nc.tensor.transpose(back[:, cols], turned[(t, c)][:, cols], identity[:])
+            nc.scalar.copy(y[c][:, t, :], back[:])
+            store(t, c)
 
         def round_part(lo, w, on_scalar):
             rounded = sb([P, PACK * w], BF16, "y_bf%d" % lo)
             dst = rounded[:].rearrange("p (c i t) -> p c t i", i=2, t=PACK)
-            src = y[:, :, lo : lo + w].rearrange("p t (c i) -> p c t i", i=2)
+            src = y[lo // HALF][:, :, lo % HALF : lo % HALF + w].rearrange("p t (c i) -> p c t i", i=2)
             if on_scalar:
                 nc.scalar.copy(dst, src)
             else:
@@ -244,50 +243,69 @@ def tile_list_hwayt_tanhP_kernel(
             return rounded
 
         def quantise_part(lo, w, rounded):
-            codes = sb([P, w], U32, "y_codes%d" % lo)
             nc.vector.quantize_mx(
-                out=codes[:].bitcast(FP8X4), scales=y_scales[:, lo : lo + w], in_=rounded[:]
+                out=y_codes[:, lo : lo + w].bitcast(FP8X4), scales=y_scales[:, lo : lo + w], in_=rounded[:]
             )
-            nc.sync.dma_start(word_rows[:, 4 * lo : 4 * (lo + w)].bitcast(I32), codes[:].bitcast(I32))
 
-        for t in range(PACK - 1):
-            if t > 0:
-                for c in range(2):
-                    pick(t, c * HALF, HALF)
-            for c in range(2):
-                mix(t, c * HALF, HALF)
-            for c in range(2):
-                if (t, c) in ON_TENSOR:
-                    finish_on_tensor(t, c)
-                else:
-                    finish(t, c * HALF, HALF)
-                store(t, c * HALF, HALF)
+        def store_codes(lo, w):
+            nc.sync.dma_start(
+                word_rows[:, 4 * lo : 4 * (lo + w)].bitcast(I32), y_codes[:, lo : lo + w].bitcast(I32)
+            )
 
-        last = PACK - 1
-        mix(last, 0, J)
-        rounded = {}
+        pick(0, 0)
+        pick(0, 1)
+        mix(0, 0)
+        mix(0, 1)
+        for t in (1, 2):
+            pick(t, 0)
+            mix(t, 0)
+        sum_turned(0, 0, 4)
+        sum_turned(0, 1, 5)
+        make(3, 0, 4)
+        mix(3, 0)
+        pick(3, 0)
+        turn_back(0, 0, 0)
+        turn_back(0, 1, 1)
+        sum_turned(1, 0, 5)
+        sum_turned(2, 0, 4)
+        make(2, 1, 0)
+        turn_back(1, 0, 2)
+        sum_turned(3, 0, 5)
+        turn_back(2, 0, 7)
+        turn_back(3, 0, 3)
+        make(3, 1, 4)
 
-        def close(n):
-            finish(last, n * PIECE, PIECE)
-            store(last, n * PIECE, PIECE)
-            if n < 3:
-                rounded[n] = round_part(n * PIECE, PIECE, True)
-
-        pick(last, 0, PIECE)
-        pick(last, PIECE, PIECE)
-        close(0)
-        pick(last, 2 * PIECE, PIECE)
-        close(1)
-        pick(last, 3 * PIECE, PIECE)
-        close(2)
+        late = sb([P, 4 * HALF], F32, "late", "carry30")
+        for n, t in enumerate((1, 2)):
+            kept[(t, 1)] = late[:, 2 * n * HALF : (2 * n + 1) * HALF]
+            mixed[(t, 1)] = late[:, (2 * n + 1) * HALF : (2 * n + 2) * HALF]
+        pick(1, 1)
+        mix(1, 1)
+        sum_turned(1, 1, 5)
+        rounded = [round_part(n * PIECE, PIECE, True) for n in range(2)]
+        turn_back(1, 1, 6)
+        pick(2, 1)
+        mix(2, 1)
+        mix(3, 1)
+        pick(3, 1, 0, PIECE)
+        finish(2, 1)
+        store(2, 1)
+        pick(3, 1, PIECE, PIECE)
+        finish(3, 1, 0, PIECE)
+        rounded.append(round_part(HALF, PIECE, True))
+        y_codes = sb([P, J], U32, "y_codes", "wg_bf11")
         quantise_part(0, PIECE, rounded[0])
-        close(3)
+        finish(3, 1, PIECE, PIECE)
+        store(3, 1)
         quantise_part(PIECE, PIECE, rounded[1])
+        store_codes(0, HALF)
         high = round_part(896, 128, False)
         low = round_part(768, 128, True)
-        quantise_part(2 * PIECE, PIECE, rounded[2])
+        quantise_part(HALF, PIECE, rounded[2])
+        store_codes(HALF, PIECE)
         quantise_part(896, 128, high)
         quantise_part(768, 128, low)
+        store_codes(3 * PIECE, PIECE)
         for q in range(4):
             queue = nc.scalar if q % 2 else nc.sync
             queue.dma_start(

@@ -299,12 +299,10 @@ def tile_list_hwayt_tanhP_kernel(
         store(3, 1)
         quantise_part(PIECE, PIECE, rounded[1])
         store_codes(0, HALF)
-        high = round_part(896, 128, False)
-        low = round_part(768, 128, True)
+        last = round_part(3 * PIECE, PIECE, False)
         quantise_part(HALF, PIECE, rounded[2])
         store_codes(HALF, PIECE)
-        quantise_part(896, 128, high)
-        quantise_part(768, 128, low)
+        quantise_part(3 * PIECE, PIECE, last)
         store_codes(3 * PIECE, PIECE)
         for q in range(4):
             queue = nc.scalar if q % 2 else nc.sync

@@ -42,13 +42,9 @@ def tile_list_hwayt_tanhP_kernel(
         nc.sync.dma_start(offsets[:], offs)
 
         scale_win = sb([P, T], U8, "scale_win")
-        nc.sync.dma_start(scale_win[12:28, :].bitcast(I32), tab_scales[1].bitcast(I32))
-        for q in range(4):
-            nc.vector.memset(scale_win[32 * q : 32 * q + (28 if q else 12), :].bitcast(I32), 0)
-            nc.sync.dma_start(
-                scale_win[32 * q + 28 : 32 * q + 32, :].bitcast(I32),
-                tab_scales[0, 4 * q : 4 * q + 4, :].bitcast(I32),
-            )
+        nc.sync.dma_start(scale_win[0:32, :].bitcast(I32), tab_scales.bitcast(I32).rearrange("a q t -> q a t"))
+        nc.vector.memset(scale_win[32:64, :].bitcast(I32), 0)
+        nc.vector.memset(scale_win[64:128, :].bitcast(I32), 0)
         planes = sb([P, PASSES * J], U8, "planes")
         nc.gpsimd.memset(planes[:].bitcast(I32), 0)
 
@@ -82,11 +78,9 @@ def tile_list_hwayt_tanhP_kernel(
 
         picked_scales = sb([P, J], U8, "picked_scales")
         nc.vector.tensor_copy(picked_scales[:], scale_win[:].indirect(offsets[:]))
-        nc.sync.dma_start(planes[0:100, 0:J].bitcast(I32), picked_scales[28:128, :].bitcast(I32))
-        for q in range(4):
+        for q in (0, 2, 1, 3):
             nc.sync.dma_start(
-                planes[32 * q : 32 * q + 4, J : 2 * J].bitcast(I32),
-                picked_scales[12 + 4 * q : 16 + 4 * q, :].bitcast(I32),
+                planes[32 * q : 32 * q + 4, :].bitcast(I32), picked_scales[8 * q : 8 * q + 8, :].bitcast(I32)
             )
 
         wh_raw = [load_weight(wh, 0, "wh_raw0", "scale_win")]

@@ -132,7 +132,7 @@ def tile_list_hwayt_tanhP_kernel(
 
         blocks = [(t, c) for t in range(PACK) for c in range(2)]
         carry = {b: half("carry", *b) for b in blocks}
-        neg_made = [sb([P, J], F32, "neg_made%d" % t) for t in range(PACK)]
+        neg_made = {}
         kept = {(t, c): half("kept", t, c) for t in range(PACK) for c in range(2) if (t, c) not in [(1, 1), (2, 1)]}
         mixed = {b: half("mixed", *b) for b in blocks if b not in [(1, 1), (2, 1)]}
 
@@ -173,13 +173,15 @@ def tile_list_hwayt_tanhP_kernel(
         gate(2)
         gate(3)
 
-        def make(t, c, b):
-            acc = product(b, wh_q, t, c)
-            nc.scalar.activation(neg_made[t][:, c * HALF : (c + 1) * HALF], acc[:], ACT.Tanh, scale=-1.0)
+        def make(t, c, tag=None):
+            neg_made[(t, c)] = half("neg_made", t, c, tag)
+            nc.scalar.activation(neg_made[(t, c)][:], made[(t, c)][:], ACT.Tanh, scale=-1.0)
 
-        for n, (t, c) in enumerate(blocks[:4]):
-            make(t, c, 4 + n)
-        make(2, 0, 6)
+        made = {}
+        for n, (t, c) in enumerate([(0, 0), (0, 1), (1, 0), (1, 1), (2, 0), (3, 0), (2, 1), (3, 1)]):
+            made[(t, c)] = product((4 + n) % 8, wh_q, t, c, (1, 0) if t > 1 else (0, 1))
+        for t, c in [(0, 0), (0, 1), (1, 0), (2, 0), (3, 0)]:
+            make(t, c)
 
         y = [sb([P, PACK, HALF], F32, "y%d" % c) for c in range(2)]
         y_rows = out_0.rearrange("(p t) j -> p t j", t=PACK)
@@ -187,9 +189,8 @@ def tile_list_hwayt_tanhP_kernel(
         word_rows = out_1[0].rearrange("p j b -> p (j b)")
 
         def mix(t, c):
-            cols = slice(c * HALF, (c + 1) * HALF)
             nc.vector.scalar_tensor_tensor(
-                mixed[(t, c)][:, :], carry[(t, c)][:], 1.0, neg_made[t][:, cols], ALU.subtract, ALU.mult
+                mixed[(t, c)][:, :], carry[(t, c)][:], 1.0, neg_made[(t, c)][:], ALU.subtract, ALU.mult
             )
 
         def finish(t, c, lo=0, w=HALF):
@@ -253,21 +254,21 @@ def tile_list_hwayt_tanhP_kernel(
         for t in (1, 2):
             pick(t, 0)
             mix(t, 0)
-        sum_turned(0, 0, 4)
-        sum_turned(0, 1, 5)
-        make(3, 0, 4)
         mix(3, 0)
         pick(3, 0)
-        turn_back(0, 0, 0)
-        turn_back(0, 1, 1)
-        sum_turned(1, 0, 5)
+        sum_turned(0, 0, 4)
+        sum_turned(0, 1, 5)
+        make(1, 1, "mixed01")
+        turn_back(0, 0, 6)
+        turn_back(0, 1, 0)
+        sum_turned(1, 0, 1)
+        make(2, 1, "mixed10")
         sum_turned(2, 0, 4)
-        make(2, 1, 0)
-        turn_back(1, 0, 2)
-        sum_turned(3, 0, 5)
-        turn_back(2, 0, 7)
-        turn_back(3, 0, 3)
-        make(3, 1, 4)
+        turn_back(1, 0, 5)
+        make(3, 1, "turned10")
+        sum_turned(3, 0, 7)
+        turn_back(2, 0, 6)
+        turn_back(3, 0, 0)
 
         late = sb([P, 4 * HALF], F32, "late", "carry30")
         for n, t in enumerate((1, 2)):
@@ -275,10 +276,10 @@ def tile_list_hwayt_tanhP_kernel(
             mixed[(t, 1)] = late[:, (2 * n + 1) * HALF : (2 * n + 2) * HALF]
         pick(1, 1)
         mix(1, 1)
-        sum_turned(1, 1, 5)
         rounded = [round_part(n * PIECE, PIECE, True) for n in range(2)]
-        turn_back(1, 1, 6)
         pick(2, 1)
+        finish(1, 1)
+        store(1, 1)
         mix(2, 1)
         mix(3, 1)
         pick(3, 1, 0, PIECE)

@@ -73,6 +73,8 @@ def tile_list_hwayt_tanhP_kernel(
         wg_raw = [load_weight(wg, a, "wg_raw%d" % a) for a in range(PASSES)]
         bias = sb([P, PACK], F32, "bias")
         nc.scalar.dma_start(bias[:], bg.rearrange("(p t) -> p t", t=PACK))
+        warm = sb([P, 1], F32, "warm")
+        nc.scalar.activation(warm[:], bias[:, 0:1], ACT.Sigmoid)
         neg_bias = sb([P, PACK], F32, "neg_bias")
         nc.scalar.mul(neg_bias[:], bias[:], -1.0)
 

from contextlib import ExitStack

import concourse.mybir as mybir
from concourse.masks import make_identity

K, N, T, J = 1024, 512, 2048, 1024
FLOPS = 2 * 2 * K * N * J

F32 = mybir.dt.float32
BF16 = mybir.dt.bfloat16
I32 = mybir.dt.int32
U32 = mybir.dt.uint32
U16 = mybir.dt.uint16
U8 = mybir.dt.uint8
FP8X4 = mybir.dt.float8_e4m3fn_x4
FP4X4 = mybir.dt.float4_e2m1fn_x4
ALU = mybir.AluOpType
ACT = mybir.ActivationFunctionType

P = 128
PACK = 4
PASSES = 2
HALF = 512
PIECE = 256


def tile_list_hwayt_tanhP_kernel(
    tc, tab_words, tab_scales, wg, wh, bg, rT, offs, out_0, out_1, out_2
):
    nc = tc.nc
    with ExitStack() as ctx:
        keep = ctx.enter_context(tc.tile_pool(name="keep", bufs=1))
        psum = ctx.enter_context(tc.psum_pool(name="psum", bufs=1))

        def bank(b):
            return psum.tile([P, HALF], F32, name="bank%d" % b, tag="bank%d" % b)

        def sb(shape, dtype, name, tag=None):
            return keep.tile(shape, dtype, name=name, tag=tag or name, align_bytes=64)

        offsets = keep.tile([P, J // 16], U16, name="offsets")
        nc.sync.dma_start(offsets[:], offs)

        scale_win = sb([P, T], U8, "scale_win")
        nc.sync.dma_start(scale_win[0:32, :].bitcast(I32), tab_scales.bitcast(I32).rearrange("a q t -> q a t"))
        nc.vector.memset(scale_win[32:64, :].bitcast(I32), 0)
        nc.vector.memset(scale_win[64:128, :].bitcast(I32), 0)
        planes = sb([P, PASSES * J], U8, "planes")
        nc.gpsimd.memset(planes[:].bitcast(I32), 0)

        identity = sb([P, P], F32, "identity")
        make_identity(nc, identity[:])

        word_win = sb([P, T], U32, "word_win")
        nc.sync.dma_start(
            word_win[:].bitcast(I32), tab_words[0].rearrange("p t b -> p (t b)").bitcast(I32)
        )

        def load_weight(w, a, name, tag=None):
            raw = sb([P, PACK * N], F32, name, tag)
            nc.sync.dma_start(
                raw[:], w[512 * a : 512 * (a + 1), :].rearrange("(p i) n -> p (i n)", i=PACK)
            )
            return raw

        r_rows = rT.rearrange("(p t) c -> p t c", t=PACK)

        def load_r(t, tag):
            win = sb([P, T], F32, "r_win%d" % t, tag)
            nc.sync.dma_start(win[:], r_rows[:, t, :])
            return win

        wg_raw = [load_weight(wg, a, "wg_raw%d" % a) for a in range(PASSES)]
        bias = sb([P, PACK], F32, "bias")
        nc.scalar.dma_start(bias[:], bg.rearrange("(p t) -> p t", t=PACK))
        warm = sb([P, 1], F32, "warm")
        nc.scalar.activation(warm[:], bias[:, 0:1], ACT.Sigmoid)
        neg_bias = sb([P, PACK], F32, "neg_bias")
        nc.scalar.mul(neg_bias[:], bias[:], -1.0)

        picked_scales = sb([P, J], U8, "picked_scales")
        nc.vector.tensor_copy(picked_scales[:], scale_win[:].indirect(offsets[:]))
        for q in (0, 2, 1, 3):
            nc.sync.dma_start(
                planes[32 * q : 32 * q + 4, :].bitcast(I32), picked_scales[8 * q : 8 * q + 8, :].bitcast(I32)
            )

        wh_raw = [load_weight(wh, 0, "wh_raw0", "scale_win")]
        picked = sb([P, J], U32, "picked")
        nc.vector.tensor_copy(picked[:], word_win[:].indirect(offsets[:]))
        wh_raw.append(load_weight(wh, 1, "wh_raw1", "word_win"))
        parted = sb([P, PASSES * 2 * J], U8, "parted")
        nc.vector.tensor_copy(
            parted[:].bitcast(U16).rearrange("p (d j) -> p d j", d=PASSES),
            picked[:].bitcast(U16).rearrange("p (j d) -> p d j", d=PASSES),
        )
        r_win = [load_r(0, "picked")]

        def round_pair(raw, u, on_scalar, name):
            rounded = sb([P, 2 * P * PACK], BF16, name)
            dst = rounded[:].rearrange("p (t m i) -> p m i t", t=2, i=PACK)
            src = raw[:].rearrange("p (i m t) -> p m i t", i=PACK, t=PACK)[:, :, :, 2 * u : 2 * u + 2]
            if on_scalar:
                nc.scalar.copy(dst, src)
            else:
                nc.vector.tensor_copy(dst, src)
            return rounded

        def quantise_pair(rounded, name):
            codes = sb([P, 2 * P], U32, name + "_codes")
            scales = sb([P, 2 * P], U8, name + "_scales")
            nc.vector.quantize_mx(out=codes[:].bitcast(FP8X4), scales=scales[:], in_=rounded[:])
            return codes, scales

        def product(b, wq, t, c, order=(0, 1)):
            acc = bank(b)
            for a in order:
                codes, scales = wq[(a, t // 2)]
                m = slice(P * (t % 2), P * (t % 2 + 1))
                lo = a * J + c * HALF
                nc.tensor.matmul_mx(
                    out=acc[:],
                    lhsT=codes[:, m].bitcast(FP8X4),
                    lhsT_scale=scales[:, m],
                    rhs=parted[:, 2 * lo : 2 * (lo + HALF)].bitcast(FP4X4),
                    rhs_scale=planes[:, lo : lo + HALF],
                    start=(a == order[0]),
                    stop=(a == order[1]),
                )
            return acc

        def half(name, t, c, tag=None):
            return sb([P, HALF], F32, "%s%d%d" % (name, t, c), tag)

        blocks = [(t, c) for t in range(PACK) for c in range(2)]
        carry = {b: half("carry", *b) for b in blocks}
        neg_made = {}
        kept = {(t, c): half("kept", t, c) for t in range(PACK) for c in range(2) if (t, c) not in [(1, 1), (2, 1)]}
        mixed = {b: half("mixed", *b) for b in blocks if b not in [(1, 1), (2, 1)]}

        wg_bf = {(0, u): round_pair(wg_raw[0], u, True, "wg_bf0%d" % u) for u in range(2)}
        r_win.append(load_r(1, "wg_raw0"))
        wg_q = {(0, 0): quantise_pair(wg_bf[(0, 0)], "wg_q00")}
        wg_bf[(1, 0)] = round_pair(wg_raw[1], 0, False, "wg_bf10")
        wg_q[(0, 1)] = quantise_pair(wg_bf[(0, 1)], "wg_q01")
        wg_q[(1, 0)] = quantise_pair(wg_bf[(1, 0)], "wg_q10")
        wg_bf[(1, 1)] = round_pair(wg_raw[1], 1, False, "wg_bf11")
        r_win.append(load_r(2, "wg_raw1"))
        wg_q[(1, 1)] = quantise_pair(wg_bf[(1, 1)], "wg_q11")
        r_win.append(load_r(3, "wg_bf11"))

        def gate(t):
            for c in range(2):
                acc = product((2 * t + c) % 4, wg_q, t, c, (1, 0) if t else (0, 1))
                nc.scalar.activation(
                    carry[(t, c)][:], acc[:], ACT.Sigmoid, bias=neg_bias[:, t : t + 1], scale=-1.0
                )

        def pick(t, c, lo=0, w=HALF):
            at = c * HALF + lo
            nc.vector.tensor_tensor(
                kept[(t, c)][:, lo : lo + w],
                r_win[t][:].indirect(offsets[:, at // 16 : (at + w) // 16]),
                carry[(t, c)][:, lo : lo + w],
                ALU.mult,
            )

        gate(0)
        gate(1)
        wh_q = {}
        for a in range(PASSES):
            wh_bf = [round_pair(wh_raw[a], u, False, "wh_bf%d%d" % (a, u)) for u in range(2)]
            for u in range(2):
                wh_q[(a, u)] = quantise_pair(wh_bf[u], "wh_q%d%d" % (a, u))
        gate(2)
        gate(3)

        def make(t, c, tag=None):
            neg_made[(t, c)] = half("neg_made", t, c, tag)
            nc.scalar.activation(neg_made[(t, c)][:], made[(t, c)][:], ACT.Tanh, scale=-1.0)

        made = {}
        for n, (t, c) in enumerate([(0, 0), (0, 1), (1, 0), (1, 1), (2, 0), (3, 0), (2, 1), (3, 1)]):
            made[(t, c)] = product((4 + n) % 8, wh_q, t, c, (1, 0) if t > 1 else (0, 1))
        for t, c in [(0, 0), (0, 1), (1, 0), (2, 0), (3, 0)]:
            make(t, c)

        y = [sb([P, PACK, HALF], F32, "y%d" % c) for c in range(2)]
        y_rows = out_0.rearrange("(p t) j -> p t j", t=PACK)
        y_scales = sb([P, J], U8, "y_scales")
        word_rows = out_1[0].rearrange("p j b -> p (j b)")

        def mix(t, c):
            nc.vector.scalar_tensor_tensor(
                mixed[(t, c)][:, :], carry[(t, c)][:], 1.0, neg_made[(t, c)][:], ALU.subtract, ALU.mult
            )

        def finish(t, c, lo=0, w=HALF):
            nc.vector.tensor_tensor(
                y[c][:, t, lo : lo + w], kept[(t, c)][:, lo : lo + w], mixed[(t, c)][:, lo : lo + w], ALU.add
            )

        def store(t, c):
            nc.sync.dma_start(y_rows[:, t, c * HALF : (c + 1) * HALF], y[c][:, t, :])

        turned = {}

        def sum_turned(t, c, b):
            summed = bank(b)
            for k in range(PACK):
                cols = slice(k * P, (k + 1) * P)
                for n, term in enumerate((kept[(t, c)], mixed[(t, c)])):
                    nc.tensor.matmul(
                        summed[:, k * P : (k + 1) * P],
                        lhsT=term[:, cols],
                        rhs=identity[:],
                        is_transpose=True,
                        start=(n == 0),
                        stop=(n == 1),
                    )
            turned[(t, c)] = half("turned", t, c)
            nc.scalar.copy(turned[(t, c)][:], summed[:])

        def turn_back(t, c, b):
            back = bank(b)
            for k in range(PACK):
                cols = slice(k * P, (k + 1) * P)
                nc.tensor.transpose(back[:, cols], turned[(t, c)][:, cols], identity[:])
            nc.scalar.copy(y[c][:, t, :], back[:])
            store(t, c)

        def round_part(lo, w, on_scalar):
            rounded = sb([P, PACK * w], BF16, "y_bf%d" % lo)
            dst = rounded[:].rearrange("p (c i t) -> p c t i", i=2, t=PACK)
            src = y[lo // HALF][:, :, lo % HALF : lo % HALF + w].rearrange("p t (c i) -> p c t i", i=2)
            if on_scalar:
                nc.scalar.copy(dst, src)
            else:
                nc.vector.tensor_copy(dst, src)
            return rounded

        def quantise_part(lo, w, rounded):
            nc.vector.quantize_mx(
                out=y_codes[:, lo : lo + w].bitcast(FP8X4), scales=y_scales[:, lo : lo + w], in_=rounded[:]
            )

        def store_codes(lo, w):
            nc.sync.dma_start(
                word_rows[:, 4 * lo : 4 * (lo + w)].bitcast(I32), y_codes[:, lo : lo + w].bitcast(I32)
            )

        pick(0, 0)
        pick(0, 1)
        mix(0, 0)
        mix(0, 1)
        for t in (1, 2):
            pick(t, 0)
            mix(t, 0)
        mix(3, 0)
        pick(3, 0)
        sum_turned(0, 0, 4)
        sum_turned(0, 1, 5)
        make(1, 1, "mixed01")
        turn_back(0, 0, 6)
        turn_back(0, 1, 0)
        sum_turned(1, 0, 1)
        make(2, 1, "mixed10")
        sum_turned(2, 0, 4)
        turn_back(1, 0, 5)
        make(3, 1, "turned10")
        sum_turned(3, 0, 7)
        turn_back(2, 0, 6)
        turn_back(3, 0, 0)

        late = sb([P, 4 * HALF], F32, "late", "carry30")
        for n, t in enumerate((1, 2)):
            kept[(t, 1)] = late[:, 2 * n * HALF : (2 * n + 1) * HALF]
            mixed[(t, 1)] = late[:, (2 * n + 1) * HALF : (2 * n + 2) * HALF]
        pick(1, 1)
        mix(1, 1)
        rounded = [round_part(n * PIECE, PIECE, True) for n in range(2)]
        pick(2, 1)
        finish(1, 1)
        store(1, 1)
        mix(2, 1)
        mix(3, 1)
        pick(3, 1, 0, PIECE)
        finish(2, 1)
        store(2, 1)
        pick(3, 1, PIECE, PIECE)
        finish(3, 1, 0, PIECE)
        rounded.append(round_part(HALF, PIECE, True))
        y_codes = sb([P, J], U32, "y_codes", "wg_bf11")
        quantise_part(0, PIECE, rounded[0])
        finish(3, 1, PIECE, PIECE)
        store(3, 1)
        quantise_part(PIECE, PIECE, rounded[1])
        store_codes(0, HALF)
        last = round_part(3 * PIECE, PIECE, False)
        quantise_part(HALF, PIECE, rounded[2])
        store_codes(HALF, PIECE)
        quantise_part(3 * PIECE, PIECE, last)
        store_codes(3 * PIECE, PIECE)
        for q in range(4):
            queue = nc.scalar if q % 2 else nc.sync
            queue.dma_start(
                out_2[0][4 * q : 4 * q + 4, :].bitcast(I32), y_scales[32 * q : 32 * q + 4, :].bitcast(I32)
            )
